import numpy as np
import ml_dtypes


def mxq(x, axis, fmt="e4m3"):
    dtype, down = {"e4m3": (ml_dtypes.float8_e4m3fn, 7), "e5m2": (ml_dtypes.float8_e5m2, 14)}[fmt]
    v = np.moveaxis(np.asarray(x, np.float32).astype(ml_dtypes.bfloat16).astype(np.float64), axis, -1)
    blocks = v.reshape(v.shape[:-1] + (-1, 32))
    amax = np.abs(blocks).max(-1, keepdims=True)
    byte = np.maximum(np.where(amax > 0, np.frexp(amax)[1] - 1 + 127, 0) - down, 1)
    scale = np.exp2(byte - 127.0)
    codes = (blocks / scale).astype(np.float32).astype(dtype).astype(np.float64)
    return np.moveaxis((codes * scale).reshape(v.shape), -1, axis)


WIDE = False


def mx_kscale(k, group=512):
    if not WIDE:
        return np.ones(k)
    levels = np.array([10, -10, 5, -5, 0])
    if group != 512:
        return np.exp2(np.random.permutation(np.resize(levels, k // group))).repeat(group)
    if k % 512:
        return np.exp2(np.random.permutation(np.resize(levels, k // 32))).repeat(32)
    a = np.empty((k // 512, 16))
    for p in range(k // 512):
        a[p, :8] = np.random.permutation(np.resize(levels, 8))
        for g in range(8):
            far = levels[np.abs(levels - a[p, g]) >= 10]
            a[p, g + 8] = far[np.random.randint(len(far))]
    return np.exp2(a.ravel()).repeat(32)


def f64(x):
    return np.asarray(x).astype(np.float64)


def striped(idx):
    return np.tile(np.asarray(idx).reshape(-1, 16).T, (8, 1)).astype(np.uint16)


def unstriped(offs):
    return offs[:16].T.reshape(-1).astype(np.int64)


H, KV, D, NQ, N = 2, 2, 256, 512, 512
CAP = 2.0


def setup_inputs():
    n = np.random.standard_normal
    s = mx_kscale(D, 0)[:, None]
    u = mx_kscale(N)
    t = np.random.uniform(0.5, 2.0, N) * u
    v = n((KV, N, 128))
    return {
        "qT": (n((H, D, NQ)) * s * (0.70 / np.sqrt(D))).astype(np.float32),
        "kT": (n((KV, D, N)) / s).astype(np.float32),
        "t": t.reshape(N, 1).astype(np.float32),
        "v": (v / t[:, None]).astype(np.float32),
        "kb": (0.5 * n((N, 1))).astype(np.float32),
    }


def reference(qT, kT, t, v, kb):
    a = mxq(f64(kT), 1, "e4m3").transpose(0, 2, 1) @ mxq(f64(qT), 1, "e4m3")
    a = a + f64(kb)
    a = CAP * np.tanh(a / CAP)
    p = a / (1.0 + np.exp(-a))
    w = p * f64(t)
    y = mxq(w, 1, "e4m3").transpose(0, 2, 1) @ mxq(f64(v), 1, "e4m3")
    y = y / 16.0
    return y

@@ -1,0 +1,244 @@
+from contextlib import ExitStack
+
+import concourse.mybir as mybir
+
+H, D, NQ, N, E = 2, 256, 512, 512, 128
+FLOPS = 2 * H * N * NQ * D + 2 * H * NQ * N * E
+
+F32 = mybir.dt.float32
+BF16 = mybir.dt.bfloat16
+U32 = mybir.dt.uint32
+U8 = mybir.dt.uint8
+FP8X4 = mybir.dt.float8_e4m3fn_x4
+ACT = mybir.ActivationFunctionType
+ALU = mybir.AluOpType
+
+P = 128
+ROWS = 64
+PACK = 4
+QT = 128
+RUN = 4
+
+
+def tile_rows_a_silu_kb_cap_kernel(tc, qT, kT, t, v, kb, out):
+    nc = tc.nc
+    with ExitStack() as ctx:
+        sb = ctx.enter_context(tc.tile_pool(name="sb", bufs=1))
+        ps = ctx.enter_context(tc.psum_pool(name="ps", bufs=1))
+        ctx.enter_context(tc.manual_schedule())
+
+        def tile(name, shape, dtype):
+            return sb.tile(shape, dtype, name=name, align_bytes=64)
+
+        def quantize(name, src, words):
+            codes = tile(name + "_codes", [P, words], U32)
+            scales = tile(name + "_scales", [P, words], U8)
+            nc.vector.quantize_mx(out=codes[:].bitcast(FP8X4), scales=scales[:], in_=src)
+            return codes, scales
+
+        k_rows = kT.rearrange("h (p j) n -> (h p) j n", j=PACK)
+        q_rows = qT.rearrange("h (p j) n -> (h p) j n", j=PACK)
+        k_raw = [tile("k_raw%d" % a, [P, 2, N], F32) for a in range(2)]
+        q_raw0 = tile("q_raw0", [P, PACK, QT], F32)
+        q_raw1 = [tile("q_raw1_%d" % a, [P, 2, NQ - QT], F32) for a in range(2)]
+        v_raw = tile("v_raw", [P, H, PACK, E], F32)
+        kb_sb = tile("kb_sb", [P, PACK], F32)
+        t_sb = tile("t_sb", [P, PACK], F32)
+        nc.sync.dma_start(out=q_raw0[:], in_=q_rows[:, :, 0:QT])
+        for a in range(2):
+            nc.sync.dma_start(out=k_raw[a][:], in_=k_rows[:, 2 * a : 2 * a + 2, :])
+        for a in range(2):
+            nc.sync.dma_start(out=q_raw1[a][:], in_=q_rows[:, 2 * a : 2 * a + 2, QT:NQ])
+        nc.sync.dma_start(out=v_raw[:], in_=v.rearrange("h (p j) e -> p h j e", j=PACK))
+        nc.scalar.dma_start(out=kb_sb[:], in_=kb.rearrange("(p j) o -> p (j o)", j=PACK))
+        nc.scalar.dma_start(out=t_sb[:], in_=t.rearrange("(p j) o -> p (j o)", j=PACK))
+
+        zero = tile("zero", [P, 1], F32)
+        warm = tile("warm", [P, 1], F32)
+        nc.vector.memset(zero[:], 0.0)
+        nc.scalar.activation(out=warm[:], in_=zero[:], func=ACT.Silu)
+
+        kb_half = tile("kb_half", [P, PACK], F32)
+        nc.vector.tensor_scalar(out=kb_half[:], in0=kb_sb[:], scalar1=0.5, scalar2=None, op0=ALU.mult)
+
+        k_bf = [tile("k_bf%d" % g, [P, 2, P, PACK], BF16) for g in range(2)]
+
+        def k_cast(a, g):
+            dst = k_bf[g][:, :, :, 2 * a : 2 * a + 2].rearrange("p r s j -> p s j r")
+            src = k_raw[a][:].rearrange("p j (s r) -> p s j r", r=PACK)[:, :, :, 2 * g : 2 * g + 2]
+            if g == 0:
+                nc.vector.tensor_copy(out=dst, in_=src)
+            else:
+                nc.scalar.copy(out=dst, in_=src)
+
+        def interleave(name, raw, cols):
+            grouped = tile(name, [P, cols, PACK], BF16)
+            nc.vector.tensor_copy(
+                out=grouped[:].rearrange("p (c i) j -> p c j i", i=RUN),
+                in_=raw.rearrange("p j (c i) -> p c j i", i=RUN),
+            )
+            return grouped[:].rearrange("p c j -> p (c j)")
+
+        q_bf0 = interleave("q_bf0", q_raw0[:], QT)
+        q_mx0 = quantize("q0", q_bf0, QT)
+        for a in range(2):
+            for g in range(2):
+                k_cast(a, g)
+        k_mx = []
+        for r in range(2):
+            k_mx.append(quantize("k%d" % r, k_bf[0][:, r].rearrange("p s j -> p (s j)"), P))
+        k_hi = quantize("k_hi", k_bf[1][:].rearrange("p r s j -> p (r s j)"), 2 * P)
+
+        banks = [[ps.tile([P, 512], F32, name="score%d_%d" % (h, b)) for b in range(3)] for h in range(H)]
+        y_banks = [ps.tile([P, 512], F32, name="y%d" % b) for b in range(2)]
+
+        def scores(h, r, q_mx, q_col, dst):
+            rows = slice(ROWS * h, ROWS * (h + 1))
+            k_codes, k_scales = k_mx[r] if r < 2 else k_hi
+            k_cols = slice(0, P) if r < 3 else slice(P, 2 * P)
+            q_codes, q_scales = q_mx
+            q_cols = slice(q_col, q_col + QT)
+            nc.tensor.matmul_mx(
+                out=dst,
+                lhsT=k_codes[rows, k_cols].bitcast(FP8X4),
+                lhsT_scale=k_scales[rows, k_cols],
+                rhs=q_codes[rows, q_cols].bitcast(FP8X4),
+                rhs_scale=q_scales[rows, q_cols],
+                start=True,
+                stop=True,
+            )
+
+        capped = [tile("capped%d" % h, [P, PACK, NQ], F32) for h in range(H)]
+
+        def cap(h, r, src, q0, q1):
+            nc.scalar.activation(
+                out=capped[h][:, r, q0:q1], in_=src, func=ACT.Tanh, bias=kb_half[:, r : r + 1], scale=0.5
+            )
+
+        p_tiles = {}
+
+        def silu(h, x):
+            p_tiles[h, x] = tile("p%d_%d" % (h, x), [P, PACK, QT], F32)
+            nc.scalar.activation(
+                out=p_tiles[h, x][:], in_=capped[h][:, :, QT * x : QT * (x + 1)], func=ACT.Silu, scale=2.0
+            )
+
+        w_bf = {}
+
+        def weigh(h, x):
+            w_bf[h, x] = tile("w%d_%d" % (h, x), [P, QT, PACK], BF16)
+            nc.vector.tensor_tensor(
+                out=w_bf[h, x][:].rearrange("p (c i) r -> p c r i", i=RUN),
+                in0=p_tiles[h, x][:].rearrange("p r (c i) -> p c r i", i=RUN),
+                in1=t_sb[:].unsqueeze(1).unsqueeze(3).to_broadcast([P, QT // RUN, PACK, RUN]),
+                op=ALU.mult,
+            )
+
+        y_ps = {}
+
+        def second(h, x):
+            w_codes, w_scales = quantize("wq%d_%d" % (h, x), w_bf[h, x][:].rearrange("p q r -> p (q r)"), QT)
+            u = len(y_ps)
+            y_ps[h, x] = y_banks[u % 2][:, E * (u // 2) : E * (u // 2 + 1)]
+            v_cols = slice(E * h, E * (h + 1))
+            nc.tensor.matmul_mx(
+                out=y_ps[h, x],
+                lhsT=w_codes[:].bitcast(FP8X4),
+                lhsT_scale=w_scales[:],
+                rhs=v_mx[0][:, v_cols].bitcast(FP8X4),
+                rhs_scale=v_mx[1][:, v_cols],
+                start=True,
+                stop=True,
+            )
+
+        def leave(h, x, on_scalar):
+            y_sb = tile("y_sb%d_%d" % (h, x), [P, E], F32)
+            if on_scalar:
+                nc.scalar.activation(out=y_sb[:], in_=y_ps[h, x], func=ACT.Copy, scale=1.0 / 16.0)
+            else:
+                nc.vector.tensor_scalar(
+                    out=y_sb[:], in0=y_ps[h, x], scalar1=1.0 / 16.0, scalar2=None, op0=ALU.mult
+                )
+            nc.sync.dma_start(out=out[h, QT * x : QT * (x + 1), :], in_=y_sb[:])
+
+        first_place = [(0, 0), (1, 0), (2, 0), (2, QT)]
+        for r in range(PACK):
+            for h in range(H):
+                b, col = first_place[r]
+                scores(h, r, q_mx0, 0, banks[h][b][:, col : col + QT])
+        for r in range(PACK):
+            for h in range(H):
+                b, col = first_place[r]
+                cap(h, r, banks[h][b][:, col : col + QT], 0, QT)
+
+        q_bf1 = tile("q_bf1", [P, QT, PACK], BF16)
+        q_bf2 = tile("q_bf2", [P, 2 * QT, PACK], BF16)
+        for a in range(2):
+            for grouped, c0, c1 in ((q_bf1, 0, QT), (q_bf2, QT, 3 * QT)):
+                nc.vector.tensor_copy(
+                    out=grouped[:, :, 2 * a : 2 * a + 2].rearrange("p (c i) j -> p c j i", i=RUN),
+                    in_=q_raw1[a][:, :, c0:c1].rearrange("p j (c i) -> p c j i", i=RUN),
+                )
+        q_mx1 = quantize("q1", q_bf1[:].rearrange("p c j -> p (c j)"), QT)
+        q_mx2 = quantize("q2", q_bf2[:].rearrange("p c j -> p (c j)"), 2 * QT)
+
+        def wide_scores(h, r):
+            bank = banks[h][r % 3]
+            scores(h, r, q_mx1, 0, bank[:, 0:QT])
+            scores(h, r, q_mx2, 0, bank[:, QT : 2 * QT])
+            scores(h, r, q_mx2, QT, bank[:, 2 * QT : 3 * QT])
+
+        def wide_cap(h, r):
+            cap(h, r, banks[h][r % 3][:, 0 : 3 * QT], QT, NQ)
+
+        silu(0, 0)
+        silu(1, 0)
+        for r in range(3):
+            wide_scores(0, r)
+        v_bf = tile("v_bf", [P, H, E, PACK], BF16)
+        nc.vector.tensor_copy(
+            out=v_bf[:].rearrange("p h (c i) j -> p h c j i", i=RUN),
+            in_=v_raw[:].rearrange("p h j (c i) -> p h c j i", i=RUN),
+        )
+        weigh(0, 0)
+        v_mx = quantize("v", v_bf[:].rearrange("p h e j -> p (h e j)"), H * E)
+        weigh(1, 0)
+        wide_cap(0, 0)
+        wide_scores(0, 3)
+        for r in range(3):
+            wide_scores(1, r)
+        second(0, 0)
+        second(1, 0)
+        for r in range(1, 4):
+            wide_cap(0, r)
+        leave(0, 0, False)
+        leave(1, 0, False)
+        wide_cap(1, 0)
+        wide_scores(1, 3)
+        silu(0, 1)
+        weigh(0, 1)
+        wide_cap(1, 1)
+        silu(0, 2)
+        weigh(0, 2)
+        second(0, 1)
+        wide_cap(1, 2)
+        silu(0, 3)
+        second(0, 2)
+        leave(0, 1, False)
+        weigh(0, 3)
+        wide_cap(1, 3)
+        leave(0, 2, False)
+        second(0, 3)
+        silu(1, 1)
+        weigh(1, 1)
+        silu(1, 2)
+        weigh(1, 2)
+        silu(1, 3)
+        second(1, 1)
+        leave(0, 3, True)
+        weigh(1, 3)
+        leave(1, 1, True)
+        second(1, 2)
+        second(1, 3)
+        leave(1, 2, True)
+        leave(1, 3, True)

@@ -17,7 +17,7 @@ P = 128
 ROWS = 64
 PACK = 4
 QT = 128
-RUN = 4
+RUN = 2
 
 
 def tile_rows_a_silu_kb_cap_kernel(tc, qT, kT, t, v, kb, out):
@@ -40,15 +40,16 @@ def tile_rows_a_silu_kb_cap_kernel(tc, qT, kT, t, v, kb, out):
         q_rows = qT.rearrange("h (p j) n -> (h p) j n", j=PACK)
         k_raw = [tile("k_raw%d" % a, [P, 2, N], F32) for a in range(2)]
         q_raw0 = tile("q_raw0", [P, PACK, QT], F32)
-        q_raw1 = [tile("q_raw1_%d" % a, [P, 2, NQ - QT], F32) for a in range(2)]
+        q_raw1 = tile("q_raw1", [P, PACK, 2 * QT], F32)
+        q_raw3 = tile("q_raw3", [P, PACK, QT], F32)
         v_raw = tile("v_raw", [P, H, PACK, E], F32)
         kb_sb = tile("kb_sb", [P, PACK], F32)
         t_sb = tile("t_sb", [P, PACK], F32)
         nc.sync.dma_start(out=q_raw0[:], in_=q_rows[:, :, 0:QT])
         for a in range(2):
             nc.sync.dma_start(out=k_raw[a][:], in_=k_rows[:, 2 * a : 2 * a + 2, :])
-        for a in range(2):
-            nc.sync.dma_start(out=q_raw1[a][:], in_=q_rows[:, 2 * a : 2 * a + 2, QT:NQ])
+        nc.sync.dma_start(out=q_raw1[:], in_=q_rows[:, :, QT : 3 * QT])
+        nc.sync.dma_start(out=q_raw3[:], in_=q_rows[:, :, 3 * QT : NQ])
         nc.sync.dma_start(out=v_raw[:], in_=v.rearrange("h (p j) e -> p h j e", j=PACK))
         nc.scalar.dma_start(out=kb_sb[:], in_=kb.rearrange("(p j) o -> p (j o)", j=PACK))
         nc.scalar.dma_start(out=t_sb[:], in_=t.rearrange("(p j) o -> p (j o)", j=PACK))
@@ -63,9 +64,9 @@ def tile_rows_a_silu_kb_cap_kernel(tc, qT, kT, t, v, kb, out):
 
         k_bf = [tile("k_bf%d" % g, [P, 2, P, PACK], BF16) for g in range(2)]
 
-        def k_cast(a, g):
-            dst = k_bf[g][:, :, :, 2 * a : 2 * a + 2].rearrange("p r s j -> p s j r")
-            src = k_raw[a][:].rearrange("p j (s r) -> p s j r", r=PACK)[:, :, :, 2 * g : 2 * g + 2]
+        def k_cast(a, g, r0, r1):
+            dst = k_bf[g][:, r0:r1, :, 2 * a : 2 * a + 2].rearrange("p r s j -> p s j r")
+            src = k_raw[a][:].rearrange("p j (s r) -> p s j r", r=PACK)[:, :, :, 2 * g + r0 : 2 * g + r1]
             if g == 0:
                 nc.vector.tensor_copy(out=dst, in_=src)
             else:
@@ -81,9 +82,11 @@ def tile_rows_a_silu_kb_cap_kernel(tc, qT, kT, t, v, kb, out):
 
         q_bf0 = interleave("q_bf0", q_raw0[:], QT)
         q_mx0 = quantize("q0", q_bf0, QT)
-        for a in range(2):
-            for g in range(2):
-                k_cast(a, g)
+        k_cast(0, 0, 0, 2)
+        k_cast(0, 1, 0, 2)
+        k_cast(1, 0, 0, 1)
+        k_cast(1, 0, 1, 2)
+        k_cast(1, 1, 0, 2)
         k_mx = []
         for r in range(2):
             k_mx.append(quantize("k%d" % r, k_bf[0][:, r].rearrange("p s j -> p (s j)"), P))
@@ -161,81 +164,93 @@ def tile_rows_a_silu_kb_cap_kernel(tc, qT, kT, t, v, kb, out):
                 )
             nc.sync.dma_start(out=out[h, QT * x : QT * (x + 1), :], in_=y_sb[:])
 
-        first_place = [(0, 0), (1, 0), (2, 0), (2, QT)]
-        for r in range(PACK):
-            for h in range(H):
-                b, col = first_place[r]
-                scores(h, r, q_mx0, 0, banks[h][b][:, col : col + QT])
-        for r in range(PACK):
-            for h in range(H):
-                b, col = first_place[r]
-                cap(h, r, banks[h][b][:, col : col + QT], 0, QT)
+        q_mx = {0: q_mx0}
 
-        q_bf1 = tile("q_bf1", [P, QT, PACK], BF16)
-        q_bf2 = tile("q_bf2", [P, 2 * QT, PACK], BF16)
-        for a in range(2):
-            for grouped, c0, c1 in ((q_bf1, 0, QT), (q_bf2, QT, 3 * QT)):
-                nc.vector.tensor_copy(
-                    out=grouped[:, :, 2 * a : 2 * a + 2].rearrange("p (c i) j -> p c j i", i=RUN),
-                    in_=q_raw1[a][:, :, c0:c1].rearrange("p j (c i) -> p c j i", i=RUN),
-                )
-        q_mx1 = quantize("q1", q_bf1[:].rearrange("p c j -> p (c j)"), QT)
-        q_mx2 = quantize("q2", q_bf2[:].rearrange("p c j -> p (c j)"), 2 * QT)
+        def place(h, r, width):
+            if width == 3:
+                return banks[h][r % 3][:, 0 : 3 * QT]
+            col = width * QT if r == 3 else 0
+            return banks[h][min(r, 2)][:, col : col + width * QT]
 
-        def wide_scores(h, r):
-            bank = banks[h][r % 3]
-            scores(h, r, q_mx1, 0, bank[:, 0:QT])
-            scores(h, r, q_mx2, 0, bank[:, QT : 2 * QT])
-            scores(h, r, q_mx2, QT, bank[:, 2 * QT : 3 * QT])
+        def chunk_scores(h, r, x0, x1):
+            dst = place(h, r, x1 - x0)
+            for x in range(x0, x1):
+                scores(h, r, q_mx[x], 0, dst[:, QT * (x - x0) : QT * (x - x0 + 1)])
 
-        def wide_cap(h, r):
-            cap(h, r, banks[h][r % 3][:, 0 : 3 * QT], QT, NQ)
+        def chunk_cap(h, r, x0, x1):
+            cap(h, r, place(h, r, x1 - x0), QT * x0, QT * x1)
 
-        silu(0, 0)
-        silu(1, 0)
-        for r in range(3):
-            wide_scores(0, r)
+        q_bf = {}
+        chunk_scores(0, 0, 0, 1)
+        chunk_scores(1, 0, 0, 1)
+        chunk_scores(0, 1, 0, 1)
+        chunk_scores(1, 1, 0, 1)
+        chunk_scores(0, 2, 0, 1)
+        chunk_scores(1, 2, 0, 1)
+        chunk_scores(0, 3, 0, 1)
+        chunk_scores(1, 3, 0, 1)
+        chunk_cap(0, 0, 0, 1)
+        chunk_cap(1, 0, 0, 1)
+        chunk_cap(0, 1, 0, 1)
+        chunk_cap(1, 1, 0, 1)
+        chunk_cap(0, 2, 0, 1)
+        chunk_cap(1, 2, 0, 1)
+        chunk_cap(0, 3, 0, 1)
+        chunk_cap(1, 3, 0, 1)
+        q_bf[1] = interleave("q_bf1", q_raw1[:, :, 0:QT], QT)
+        q_bf[2] = interleave("q_bf2", q_raw1[:, :, QT : 2 * QT], QT)
+        q_mx[1] = quantize("q1", q_bf[1], QT)
+        q_bf[3] = interleave("q_bf3", q_raw3[:], QT)
+        q_mx[2] = quantize("q2", q_bf[2], QT)
+        q_mx[3] = quantize("q3", q_bf[3], QT)
+        chunk_scores(0, 0, 1, 4)
+        chunk_scores(0, 1, 1, 4)
+        chunk_scores(0, 2, 1, 4)
+        chunk_scores(1, 0, 1, 4)
         v_bf = tile("v_bf", [P, H, E, PACK], BF16)
         nc.vector.tensor_copy(
             out=v_bf[:].rearrange("p h (c i) j -> p h c j i", i=RUN),
             in_=v_raw[:].rearrange("p h j (c i) -> p h c j i", i=RUN),
         )
+        silu(0, 0)
+        silu(1, 0)
         weigh(0, 0)
         v_mx = quantize("v", v_bf[:].rearrange("p h e j -> p (h e j)"), H * E)
         weigh(1, 0)
-        wide_cap(0, 0)
-        wide_scores(0, 3)
-        for r in range(3):
-            wide_scores(1, r)
+        chunk_cap(0, 0, 1, 4)
+        chunk_scores(0, 3, 1, 4)
+        chunk_scores(1, 1, 1, 4)
+        chunk_scores(1, 2, 1, 4)
+        chunk_cap(0, 1, 1, 4)
         second(0, 0)
         second(1, 0)
-        for r in range(1, 4):
-            wide_cap(0, r)
+        chunk_cap(0, 2, 1, 4)
+        chunk_cap(0, 3, 1, 4)
         leave(0, 0, False)
         leave(1, 0, False)
-        wide_cap(1, 0)
-        wide_scores(1, 3)
+        chunk_cap(1, 0, 1, 4)
+        chunk_scores(1, 3, 1, 4)
         silu(0, 1)
         weigh(0, 1)
-        wide_cap(1, 1)
+        chunk_cap(1, 1, 1, 4)
         silu(0, 2)
         weigh(0, 2)
         second(0, 1)
-        wide_cap(1, 2)
+        chunk_cap(1, 2, 1, 4)
         silu(0, 3)
-        second(0, 2)
-        leave(0, 1, False)
         weigh(0, 3)
-        wide_cap(1, 3)
-        leave(0, 2, False)
-        second(0, 3)
+        second(0, 2)
+        chunk_cap(1, 3, 1, 4)
+        leave(0, 1, True)
         silu(1, 1)
+        second(0, 3)
         weigh(1, 1)
         silu(1, 2)
         weigh(1, 2)
         silu(1, 3)
-        second(1, 1)
+        leave(0, 2, True)
         leave(0, 3, True)
+        second(1, 1)
         weigh(1, 3)
         leave(1, 1, True)
         second(1, 2)

@@ -17,6 +17,9 @@ P = 128
 ROWS = 64
 PACK = 4
 QT = 128
+TILES = NQ // QT
+BANK = 512
+SCORE_BANKS = 3
 RUN = 2
 
 
@@ -38,21 +41,22 @@ def tile_rows_a_silu_kb_cap_kernel(tc, qT, kT, t, v, kb, out):
 
         k_rows = kT.rearrange("h (p j) n -> (h p) j n", j=PACK)
         q_rows = qT.rearrange("h (p j) n -> (h p) j n", j=PACK)
-        k_raw = [tile("k_raw%d" % a, [P, 2, N], F32) for a in range(2)]
+        k_raw = [tile("k_raw%d" % half, [P, 2, N], F32) for half in range(2)]
         q_raw0 = tile("q_raw0", [P, PACK, QT], F32)
-        q_raw1 = tile("q_raw1", [P, PACK, 2 * QT], F32)
+        q_raw12 = tile("q_raw12", [P, PACK, 2 * QT], F32)
         q_raw3 = tile("q_raw3", [P, PACK, QT], F32)
         v_raw = tile("v_raw", [P, H, PACK, E], F32)
         kb_sb = tile("kb_sb", [P, PACK], F32)
         t_sb = tile("t_sb", [P, PACK], F32)
         nc.sync.dma_start(out=q_raw0[:], in_=q_rows[:, :, 0:QT])
-        for a in range(2):
-            nc.sync.dma_start(out=k_raw[a][:], in_=k_rows[:, 2 * a : 2 * a + 2, :])
-        nc.sync.dma_start(out=q_raw1[:], in_=q_rows[:, :, QT : 3 * QT])
+        for half in range(2):
+            nc.sync.dma_start(out=k_raw[half][:], in_=k_rows[:, 2 * half : 2 * half + 2, :])
+        nc.sync.dma_start(out=q_raw12[:], in_=q_rows[:, :, QT : 3 * QT])
         nc.sync.dma_start(out=q_raw3[:], in_=q_rows[:, :, 3 * QT : NQ])
         nc.sync.dma_start(out=v_raw[:], in_=v.rearrange("h (p j) e -> p h j e", j=PACK))
-        nc.scalar.dma_start(out=kb_sb[:], in_=kb.rearrange("(p j) o -> p (j o)", j=PACK))
-        nc.scalar.dma_start(out=t_sb[:], in_=t.rearrange("(p j) o -> p (j o)", j=PACK))
+        nc.scalar.dma_start(out=kb_sb[:], in_=kb.rearrange("(s r) o -> s (r o)", r=PACK))
+        nc.scalar.dma_start(out=t_sb[:], in_=t.rearrange("(s r) o -> s (r o)", r=PACK))
+        q_raw = [q_raw0[:], q_raw12[:, :, 0:QT], q_raw12[:, :, QT : 2 * QT], q_raw3[:]]
 
         zero = tile("zero", [P, 1], F32)
         warm = tile("warm", [P, 1], F32)
@@ -62,198 +66,190 @@ def tile_rows_a_silu_kb_cap_kernel(tc, qT, kT, t, v, kb, out):
         kb_half = tile("kb_half", [P, PACK], F32)
         nc.vector.tensor_scalar(out=kb_half[:], in0=kb_sb[:], scalar1=0.5, scalar2=None, op0=ALU.mult)
 
+        q_bf = {}
+        q_mx = {}
+
+        def round_q(x):
+            q_bf[x] = tile("q_bf%d" % x, [P, QT, PACK], BF16)
+            nc.vector.tensor_copy(
+                out=q_bf[x][:].rearrange("p (c i) j -> p c j i", i=RUN),
+                in_=q_raw[x].rearrange("p j (c i) -> p c j i", i=RUN),
+            )
+
+        def quantize_q(x):
+            q_mx[x] = quantize("q%d" % x, q_bf[x][:].rearrange("p c j -> p (c j)"), QT)
+
         k_bf = [tile("k_bf%d" % g, [P, 2, P, PACK], BF16) for g in range(2)]
 
-        def k_cast(a, g, r0, r1):
-            dst = k_bf[g][:, r0:r1, :, 2 * a : 2 * a + 2].rearrange("p r s j -> p s j r")
-            src = k_raw[a][:].rearrange("p j (s r) -> p s j r", r=PACK)[:, :, :, 2 * g + r0 : 2 * g + r1]
+        def round_k(half, r0, r1):
+            g = r0 // 2
+            dst = k_bf[g][:, r0 - 2 * g : r1 - 2 * g, :, 2 * half : 2 * half + 2].rearrange("p r s j -> p s j r")
+            src = k_raw[half][:].rearrange("p j (s r) -> p s j r", r=PACK)[:, :, :, r0:r1]
             if g == 0:
                 nc.vector.tensor_copy(out=dst, in_=src)
             else:
                 nc.scalar.copy(out=dst, in_=src)
 
-        def interleave(name, raw, cols):
-            grouped = tile(name, [P, cols, PACK], BF16)
-            nc.vector.tensor_copy(
-                out=grouped[:].rearrange("p (c i) j -> p c j i", i=RUN),
-                in_=raw.rearrange("p j (c i) -> p c j i", i=RUN),
-            )
-            return grouped[:].rearrange("p c j -> p (c j)")
-
-        q_bf0 = interleave("q_bf0", q_raw0[:], QT)
-        q_mx0 = quantize("q0", q_bf0, QT)
-        k_cast(0, 0, 0, 2)
-        k_cast(0, 1, 0, 2)
-        k_cast(1, 0, 0, 1)
-        k_cast(1, 0, 1, 2)
-        k_cast(1, 1, 0, 2)
+        round_q(0)
+        quantize_q(0)
+        round_k(0, 0, 2)
+        round_k(0, 2, 4)
+        round_k(1, 0, 1)
+        round_k(1, 1, 2)
+        round_k(1, 2, 4)
         k_mx = []
         for r in range(2):
-            k_mx.append(quantize("k%d" % r, k_bf[0][:, r].rearrange("p s j -> p (s j)"), P))
-        k_hi = quantize("k_hi", k_bf[1][:].rearrange("p r s j -> p (r s j)"), 2 * P)
+            k_mx.append(quantize("k%d" % r, k_bf[0][:, r].rearrange("p s j -> p (s j)"), P) + (0,))
+        k_late = quantize("k_late", k_bf[1][:].rearrange("p r s j -> p (r s j)"), 2 * P)
+        k_mx.extend([k_late + (0,), k_late + (P,)])
 
-        banks = [[ps.tile([P, 512], F32, name="score%d_%d" % (h, b)) for b in range(3)] for h in range(H)]
-        y_banks = [ps.tile([P, 512], F32, name="y%d" % b) for b in range(2)]
+        score_banks = [
+            [ps.tile([P, BANK], F32, name="score%d_%d" % (h, b)) for b in range(SCORE_BANKS)] for h in range(H)
+        ]
+        y_banks = [ps.tile([P, BANK], F32, name="y%d" % b) for b in range(2)]
 
-        def scores(h, r, q_mx, q_col, dst):
+        def score_psum(h, r, x0, x1):
+            if x0 == 0:
+                col = QT * (r // SCORE_BANKS)
+                return score_banks[h][min(r, SCORE_BANKS - 1)][:, col : col + QT]
+            return score_banks[h][r % SCORE_BANKS][:, QT * (x0 - 1) : QT * (x1 - 1)]
+
+        def scores(h, r, x0, x1):
             rows = slice(ROWS * h, ROWS * (h + 1))
-            k_codes, k_scales = k_mx[r] if r < 2 else k_hi
-            k_cols = slice(0, P) if r < 3 else slice(P, 2 * P)
-            q_codes, q_scales = q_mx
-            q_cols = slice(q_col, q_col + QT)
-            nc.tensor.matmul_mx(
-                out=dst,
-                lhsT=k_codes[rows, k_cols].bitcast(FP8X4),
-                lhsT_scale=k_scales[rows, k_cols],
-                rhs=q_codes[rows, q_cols].bitcast(FP8X4),
-                rhs_scale=q_scales[rows, q_cols],
-                start=True,
-                stop=True,
-            )
+            k_codes, k_scales, k_col = k_mx[r]
+            k_cols = slice(k_col, k_col + P)
+            for x in range(x0, x1):
+                q_codes, q_scales = q_mx[x]
+                nc.tensor.matmul_mx(
+                    out=score_psum(h, r, x, x + 1),
+                    lhsT=k_codes[rows, k_cols].bitcast(FP8X4),
+                    lhsT_scale=k_scales[rows, k_cols],
+                    rhs=q_codes[rows, 0:QT].bitcast(FP8X4),
+                    rhs_scale=q_scales[rows, 0:QT],
+                    start=True,
+                    stop=True,
+                )
 
-        capped = [tile("capped%d" % h, [P, PACK, NQ], F32) for h in range(H)]
+        half_c = [tile("half_c%d" % h, [P, PACK, NQ], F32) for h in range(H)]
 
-        def cap(h, r, src, q0, q1):
+        def cap(h, r, x0, x1):
             nc.scalar.activation(
-                out=capped[h][:, r, q0:q1], in_=src, func=ACT.Tanh, bias=kb_half[:, r : r + 1], scale=0.5
+                out=half_c[h][:, r, QT * x0 : QT * x1],
+                in_=score_psum(h, r, x0, x1),
+                func=ACT.Tanh,
+                bias=kb_half[:, r : r + 1],
+                scale=0.5,
             )
 
-        p_tiles = {}
+        p_sb = {}
+        w_bf = {}
 
         def silu(h, x):
-            p_tiles[h, x] = tile("p%d_%d" % (h, x), [P, PACK, QT], F32)
+            p_sb[h, x] = tile("p%d_%d" % (h, x), [P, PACK, QT], F32)
             nc.scalar.activation(
-                out=p_tiles[h, x][:], in_=capped[h][:, :, QT * x : QT * (x + 1)], func=ACT.Silu, scale=2.0
+                out=p_sb[h, x][:], in_=half_c[h][:, :, QT * x : QT * (x + 1)], func=ACT.Silu, scale=2.0
             )
-
-        w_bf = {}
 
         def weigh(h, x):
             w_bf[h, x] = tile("w%d_%d" % (h, x), [P, QT, PACK], BF16)
             nc.vector.tensor_tensor(
                 out=w_bf[h, x][:].rearrange("p (c i) r -> p c r i", i=RUN),
-                in0=p_tiles[h, x][:].rearrange("p r (c i) -> p c r i", i=RUN),
+                in0=p_sb[h, x][:].rearrange("p r (c i) -> p c r i", i=RUN),
                 in1=t_sb[:].unsqueeze(1).unsqueeze(3).to_broadcast([P, QT // RUN, PACK, RUN]),
                 op=ALU.mult,
             )
 
-        y_ps = {}
+        def y_psum(h, x0, x1):
+            if (h, x0) == (H - 1, TILES - 2):
+                return y_banks[0][:, 0:E]
+            return y_banks[h][:, E * x0 : E * x1]
 
-        def second(h, x):
+        def mix(h, x):
             w_codes, w_scales = quantize("wq%d_%d" % (h, x), w_bf[h, x][:].rearrange("p q r -> p (q r)"), QT)
-            u = len(y_ps)
-            y_ps[h, x] = y_banks[u % 2][:, E * (u // 2) : E * (u // 2 + 1)]
             v_cols = slice(E * h, E * (h + 1))
             nc.tensor.matmul_mx(
-                out=y_ps[h, x],
+                out=y_psum(h, x, x + 1),
                 lhsT=w_codes[:].bitcast(FP8X4),
                 lhsT_scale=w_scales[:],
-                rhs=v_mx[0][:, v_cols].bitcast(FP8X4),
-                rhs_scale=v_mx[1][:, v_cols],
+                rhs=v_codes[:, v_cols].bitcast(FP8X4),
+                rhs_scale=v_scales[:, v_cols],
                 start=True,
                 stop=True,
             )
 
-        def leave(h, x, on_scalar):
-            y_sb = tile("y_sb%d_%d" % (h, x), [P, E], F32)
-            if on_scalar:
-                nc.scalar.activation(out=y_sb[:], in_=y_ps[h, x], func=ACT.Copy, scale=1.0 / 16.0)
-            else:
-                nc.vector.tensor_scalar(
-                    out=y_sb[:], in0=y_ps[h, x], scalar1=1.0 / 16.0, scalar2=None, op0=ALU.mult
-                )
-            nc.sync.dma_start(out=out[h, QT * x : QT * (x + 1), :], in_=y_sb[:])
+        def leave(h, x0, x1):
+            y_sb = tile("y_sb%d_%d" % (h, x0), [P, (x1 - x0) * E], F32)
+            nc.scalar.activation(out=y_sb[:], in_=y_psum(h, x0, x1), func=ACT.Copy, scale=1.0 / 16.0)
+            nc.sync.dma_start(
+                out=out[h, QT * x0 : QT * x1, :].rearrange("(x p) e -> p x e", p=P),
+                in_=y_sb[:].rearrange("p (x e) -> p x e", e=E),
+            )
 
-        q_mx = {0: q_mx0}
+        for r in range(PACK):
+            for h in range(H):
+                scores(h, r, 0, 1)
+        for r in range(PACK):
+            for h in range(H):
+                cap(h, r, 0, 1)
 
-        def place(h, r, width):
-            if width == 3:
-                return banks[h][r % 3][:, 0 : 3 * QT]
-            col = width * QT if r == 3 else 0
-            return banks[h][min(r, 2)][:, col : col + width * QT]
+        round_q(1)
+        round_q(2)
+        quantize_q(1)
+        round_q(3)
+        quantize_q(2)
+        quantize_q(3)
+        for r in range(SCORE_BANKS):
+            scores(0, r, 1, TILES)
+        scores(1, 0, 1, TILES)
 
-        def chunk_scores(h, r, x0, x1):
-            dst = place(h, r, x1 - x0)
-            for x in range(x0, x1):
-                scores(h, r, q_mx[x], 0, dst[:, QT * (x - x0) : QT * (x - x0 + 1)])
-
-        def chunk_cap(h, r, x0, x1):
-            cap(h, r, place(h, r, x1 - x0), QT * x0, QT * x1)
-
-        q_bf = {}
-        chunk_scores(0, 0, 0, 1)
-        chunk_scores(1, 0, 0, 1)
-        chunk_scores(0, 1, 0, 1)
-        chunk_scores(1, 1, 0, 1)
-        chunk_scores(0, 2, 0, 1)
-        chunk_scores(1, 2, 0, 1)
-        chunk_scores(0, 3, 0, 1)
-        chunk_scores(1, 3, 0, 1)
-        chunk_cap(0, 0, 0, 1)
-        chunk_cap(1, 0, 0, 1)
-        chunk_cap(0, 1, 0, 1)
-        chunk_cap(1, 1, 0, 1)
-        chunk_cap(0, 2, 0, 1)
-        chunk_cap(1, 2, 0, 1)
-        chunk_cap(0, 3, 0, 1)
-        chunk_cap(1, 3, 0, 1)
-        q_bf[1] = interleave("q_bf1", q_raw1[:, :, 0:QT], QT)
-        q_bf[2] = interleave("q_bf2", q_raw1[:, :, QT : 2 * QT], QT)
-        q_mx[1] = quantize("q1", q_bf[1], QT)
-        q_bf[3] = interleave("q_bf3", q_raw3[:], QT)
-        q_mx[2] = quantize("q2", q_bf[2], QT)
-        q_mx[3] = quantize("q3", q_bf[3], QT)
-        chunk_scores(0, 0, 1, 4)
-        chunk_scores(0, 1, 1, 4)
-        chunk_scores(0, 2, 1, 4)
-        chunk_scores(1, 0, 1, 4)
+        for h in range(H):
+            silu(h, 0)
+        weigh(0, 0)
         v_bf = tile("v_bf", [P, H, E, PACK], BF16)
         nc.vector.tensor_copy(
             out=v_bf[:].rearrange("p h (c i) j -> p h c j i", i=RUN),
             in_=v_raw[:].rearrange("p h j (c i) -> p h c j i", i=RUN),
         )
-        silu(0, 0)
-        silu(1, 0)
-        weigh(0, 0)
-        v_mx = quantize("v", v_bf[:].rearrange("p h e j -> p (h e j)"), H * E)
         weigh(1, 0)
-        chunk_cap(0, 0, 1, 4)
-        chunk_scores(0, 3, 1, 4)
-        chunk_scores(1, 1, 1, 4)
-        chunk_scores(1, 2, 1, 4)
-        chunk_cap(0, 1, 1, 4)
-        second(0, 0)
-        second(1, 0)
-        chunk_cap(0, 2, 1, 4)
-        chunk_cap(0, 3, 1, 4)
-        leave(0, 0, False)
-        leave(1, 0, False)
-        chunk_cap(1, 0, 1, 4)
-        chunk_scores(1, 3, 1, 4)
+        v_codes, v_scales = quantize("v", v_bf[:].rearrange("p h e j -> p (h e j)"), H * E)
+
+        cap(0, 0, 1, TILES)
+        scores(0, 3, 1, TILES)
+        scores(1, 1, 1, TILES)
+        scores(1, 2, 1, TILES)
+        cap(0, 1, 1, TILES)
+        for h in range(H):
+            mix(h, 0)
+        cap(0, 2, 1, TILES)
+        cap(0, 3, 1, TILES)
+
+        cap(1, 0, 1, TILES)
+        scores(1, 3, 1, TILES)
         silu(0, 1)
         weigh(0, 1)
-        chunk_cap(1, 1, 1, 4)
+        cap(1, 1, 1, TILES)
         silu(0, 2)
         weigh(0, 2)
-        second(0, 1)
-        chunk_cap(1, 2, 1, 4)
+        mix(0, 1)
+        cap(1, 2, 1, 3)
         silu(0, 3)
         weigh(0, 3)
-        second(0, 2)
-        chunk_cap(1, 3, 1, 4)
-        leave(0, 1, True)
+        mix(0, 2)
+        cap(1, 3, 1, 3)
+        cap(1, 2, 3, TILES)
         silu(1, 1)
-        second(0, 3)
+        mix(0, 3)
         weigh(1, 1)
+        cap(1, 3, 3, TILES)
         silu(1, 2)
         weigh(1, 2)
         silu(1, 3)
-        leave(0, 2, True)
-        leave(0, 3, True)
-        second(1, 1)
+
+        leave(0, 0, TILES)
+        mix(1, 1)
         weigh(1, 3)
-        leave(1, 1, True)
-        second(1, 2)
-        second(1, 3)
-        leave(1, 2, True)
-        leave(1, 3, True)
+        leave(1, 0, 2)
+        mix(1, 2)
+        mix(1, 3)
+        leave(1, 2, 3)
+        leave(1, 3, TILES)

from contextlib import ExitStack

import concourse.mybir as mybir

H, D, NQ, N, E = 2, 256, 512, 512, 128
FLOPS = 2 * H * N * NQ * D + 2 * H * NQ * N * E

F32 = mybir.dt.float32
BF16 = mybir.dt.bfloat16
U32 = mybir.dt.uint32
U8 = mybir.dt.uint8
FP8X4 = mybir.dt.float8_e4m3fn_x4
ACT = mybir.ActivationFunctionType
ALU = mybir.AluOpType

P = 128
ROWS = 64
PACK = 4
QT = 128
TILES = NQ // QT
BANK = 512
SCORE_BANKS = 3
RUN = 2


def tile_rows_a_silu_kb_cap_kernel(tc, qT, kT, t, v, kb, out):
    nc = tc.nc
    with ExitStack() as ctx:
        sb = ctx.enter_context(tc.tile_pool(name="sb", bufs=1))
        ps = ctx.enter_context(tc.psum_pool(name="ps", bufs=1))
        ctx.enter_context(tc.manual_schedule())

        def tile(name, shape, dtype):
            return sb.tile(shape, dtype, name=name, align_bytes=64)

        def quantize(name, src, words):
            codes = tile(name + "_codes", [P, words], U32)
            scales = tile(name + "_scales", [P, words], U8)
            nc.vector.quantize_mx(out=codes[:].bitcast(FP8X4), scales=scales[:], in_=src)
            return codes, scales

        k_rows = kT.rearrange("h (p j) n -> (h p) j n", j=PACK)
        q_rows = qT.rearrange("h (p j) n -> (h p) j n", j=PACK)
        k_raw = [tile("k_raw%d" % half, [P, 2, N], F32) for half in range(2)]
        q_raw0 = tile("q_raw0", [P, PACK, QT], F32)
        q_raw12 = tile("q_raw12", [P, PACK, 2 * QT], F32)
        q_raw3 = tile("q_raw3", [P, PACK, QT], F32)
        v_raw = tile("v_raw", [P, H, PACK, E], F32)
        kb_sb = tile("kb_sb", [P, PACK], F32)
        t_sb = tile("t_sb", [P, PACK], F32)
        nc.sync.dma_start(out=q_raw0[:], in_=q_rows[:, :, 0:QT])
        for half in range(2):
            nc.sync.dma_start(out=k_raw[half][:], in_=k_rows[:, 2 * half : 2 * half + 2, :])
        nc.sync.dma_start(out=q_raw12[:], in_=q_rows[:, :, QT : 3 * QT])
        nc.sync.dma_start(out=q_raw3[:], in_=q_rows[:, :, 3 * QT : NQ])
        nc.sync.dma_start(out=v_raw[:], in_=v.rearrange("h (p j) e -> p h j e", j=PACK))
        nc.scalar.dma_start(out=kb_sb[:], in_=kb.rearrange("(s r) o -> s (r o)", r=PACK))
        nc.scalar.dma_start(out=t_sb[:], in_=t.rearrange("(s r) o -> s (r o)", r=PACK))
        q_raw = [q_raw0[:], q_raw12[:, :, 0:QT], q_raw12[:, :, QT : 2 * QT], q_raw3[:]]

        zero = tile("zero", [P, 1], F32)
        warm = tile("warm", [P, 1], F32)
        nc.vector.memset(zero[:], 0.0)
        nc.scalar.activation(out=warm[:], in_=zero[:], func=ACT.Silu)

        kb_half = tile("kb_half", [P, PACK], F32)
        nc.vector.tensor_scalar(out=kb_half[:], in0=kb_sb[:], scalar1=0.5, scalar2=None, op0=ALU.mult)

        q_bf = {}
        q_mx = {}

        def round_q(x):
            q_bf[x] = tile("q_bf%d" % x, [P, QT, PACK], BF16)
            nc.vector.tensor_copy(
                out=q_bf[x][:].rearrange("p (c i) j -> p c j i", i=RUN),
                in_=q_raw[x].rearrange("p j (c i) -> p c j i", i=RUN),
            )

        def quantize_q(x):
            q_mx[x] = quantize("q%d" % x, q_bf[x][:].rearrange("p c j -> p (c j)"), QT)

        k_bf = [tile("k_bf%d" % g, [P, 2, P, PACK], BF16) for g in range(2)]

        def round_k(half, r0, r1):
            g = r0 // 2
            dst = k_bf[g][:, r0 - 2 * g : r1 - 2 * g, :, 2 * half : 2 * half + 2].rearrange("p r s j -> p s j r")
            src = k_raw[half][:].rearrange("p j (s r) -> p s j r", r=PACK)[:, :, :, r0:r1]
            if g == 0:
                nc.vector.tensor_copy(out=dst, in_=src)
            else:
                nc.scalar.copy(out=dst, in_=src)

        round_q(0)
        quantize_q(0)
        round_k(0, 0, 2)
        round_k(0, 2, 4)
        round_k(1, 0, 1)
        round_k(1, 1, 2)
        round_k(1, 2, 4)
        k_mx = []
        for r in range(2):
            k_mx.append(quantize("k%d" % r, k_bf[0][:, r].rearrange("p s j -> p (s j)"), P) + (0,))
        k_late = quantize("k_late", k_bf[1][:].rearrange("p r s j -> p (r s j)"), 2 * P)
        k_mx.extend([k_late + (0,), k_late + (P,)])

        score_banks = [
            [ps.tile([P, BANK], F32, name="score%d_%d" % (h, b)) for b in range(SCORE_BANKS)] for h in range(H)
        ]
        y_banks = [ps.tile([P, BANK], F32, name="y%d" % b) for b in range(2)]

        def score_psum(h, r, x0, x1):
            if x0 == 0:
                col = QT * (r // SCORE_BANKS)
                return score_banks[h][min(r, SCORE_BANKS - 1)][:, col : col + QT]
            return score_banks[h][r % SCORE_BANKS][:, QT * (x0 - 1) : QT * (x1 - 1)]

        def scores(h, r, x0, x1):
            rows = slice(ROWS * h, ROWS * (h + 1))
            k_codes, k_scales, k_col = k_mx[r]
            k_cols = slice(k_col, k_col + P)
            for x in range(x0, x1):
                q_codes, q_scales = q_mx[x]
                nc.tensor.matmul_mx(
                    out=score_psum(h, r, x, x + 1),
                    lhsT=k_codes[rows, k_cols].bitcast(FP8X4),
                    lhsT_scale=k_scales[rows, k_cols],
                    rhs=q_codes[rows, 0:QT].bitcast(FP8X4),
                    rhs_scale=q_scales[rows, 0:QT],
                    start=True,
                    stop=True,
                )

        half_c = [tile("half_c%d" % h, [P, PACK, NQ], F32) for h in range(H)]

        def cap(h, r, x0, x1):
            nc.scalar.activation(
                out=half_c[h][:, r, QT * x0 : QT * x1],
                in_=score_psum(h, r, x0, x1),
                func=ACT.Tanh,
                bias=kb_half[:, r : r + 1],
                scale=0.5,
            )

        p_sb = {}
        w_bf = {}

        def silu(h, x):
            p_sb[h, x] = tile("p%d_%d" % (h, x), [P, PACK, QT], F32)
            nc.scalar.activation(
                out=p_sb[h, x][:], in_=half_c[h][:, :, QT * x : QT * (x + 1)], func=ACT.Silu, scale=2.0
            )

        def weigh(h, x):
            w_bf[h, x] = tile("w%d_%d" % (h, x), [P, QT, PACK], BF16)
            nc.vector.tensor_tensor(
                out=w_bf[h, x][:].rearrange("p (c i) r -> p c r i", i=RUN),
                in0=p_sb[h, x][:].rearrange("p r (c i) -> p c r i", i=RUN),
                in1=t_sb[:].unsqueeze(1).unsqueeze(3).to_broadcast([P, QT // RUN, PACK, RUN]),
                op=ALU.mult,
            )

        def y_psum(h, x0, x1):
            if (h, x0) == (H - 1, TILES - 2):
                return y_banks[0][:, 0:E]
            return y_banks[h][:, E * x0 : E * x1]

        def mix(h, x):
            w_codes, w_scales = quantize("wq%d_%d" % (h, x), w_bf[h, x][:].rearrange("p q r -> p (q r)"), QT)
            v_cols = slice(E * h, E * (h + 1))
            nc.tensor.matmul_mx(
                out=y_psum(h, x, x + 1),
                lhsT=w_codes[:].bitcast(FP8X4),
                lhsT_scale=w_scales[:],
                rhs=v_codes[:, v_cols].bitcast(FP8X4),
                rhs_scale=v_scales[:, v_cols],
                start=True,
                stop=True,
            )

        def leave(h, x0, x1):
            y_sb = tile("y_sb%d_%d" % (h, x0), [P, (x1 - x0) * E], F32)
            nc.scalar.activation(out=y_sb[:], in_=y_psum(h, x0, x1), func=ACT.Copy, scale=1.0 / 16.0)
            nc.sync.dma_start(
                out=out[h, QT * x0 : QT * x1, :].rearrange("(x p) e -> p x e", p=P),
                in_=y_sb[:].rearrange("p (x e) -> p x e", e=E),
            )

        for r in range(PACK):
            for h in range(H):
                scores(h, r, 0, 1)
        for r in range(PACK):
            for h in range(H):
                cap(h, r, 0, 1)

        round_q(1)
        round_q(2)
        quantize_q(1)
        round_q(3)
        quantize_q(2)
        quantize_q(3)
        for r in range(SCORE_BANKS):
            scores(0, r, 1, TILES)
        scores(1, 0, 1, TILES)

        for h in range(H):
            silu(h, 0)
        weigh(0, 0)
        v_bf = tile("v_bf", [P, H, E, PACK], BF16)
        nc.vector.tensor_copy(
            out=v_bf[:].rearrange("p h (c i) j -> p h c j i", i=RUN),
            in_=v_raw[:].rearrange("p h j (c i) -> p h c j i", i=RUN),
        )
        weigh(1, 0)
        v_codes, v_scales = quantize("v", v_bf[:].rearrange("p h e j -> p (h e j)"), H * E)

        cap(0, 0, 1, TILES)
        scores(0, 3, 1, TILES)
        scores(1, 1, 1, TILES)
        scores(1, 2, 1, TILES)
        cap(0, 1, 1, TILES)
        for h in range(H):
            mix(h, 0)
        cap(0, 2, 1, TILES)
        cap(0, 3, 1, TILES)

        cap(1, 0, 1, TILES)
        scores(1, 3, 1, TILES)
        silu(0, 1)
        weigh(0, 1)
        cap(1, 1, 1, TILES)
        silu(0, 2)
        weigh(0, 2)
        mix(0, 1)
        cap(1, 2, 1, 3)
        silu(0, 3)
        weigh(0, 3)
        mix(0, 2)
        cap(1, 3, 1, 3)
        cap(1, 2, 3, TILES)
        silu(1, 1)
        mix(0, 3)
        weigh(1, 1)
        cap(1, 3, 3, TILES)
        silu(1, 2)
        weigh(1, 2)
        silu(1, 3)

        leave(0, 0, TILES)
        mix(1, 1)
        weigh(1, 3)
        leave(1, 0, 2)
        mix(1, 2)
        mix(1, 3)
        leave(1, 2, 3)
        leave(1, 3, TILES)
